import numpy as np
import ml_dtypes


def mxq(x, axis, fmt="e4m3"):
    dtype, down = {"e4m3": (ml_dtypes.float8_e4m3fn, 7), "e5m2": (ml_dtypes.float8_e5m2, 14)}[fmt]
    v = np.moveaxis(np.asarray(x, np.float32).astype(ml_dtypes.bfloat16).astype(np.float64), axis, -1)
    blocks = v.reshape(v.shape[:-1] + (-1, 32))
    amax = np.abs(blocks).max(-1, keepdims=True)
    byte = np.maximum(np.where(amax > 0, np.frexp(amax)[1] - 1 + 127, 0) - down, 1)
    scale = np.exp2(byte - 127.0)
    codes = (blocks / scale).astype(np.float32).astype(dtype).astype(np.float64)
    return np.moveaxis((codes * scale).reshape(v.shape), -1, axis)


WIDE = False


def mx_kscale(k):
    if not WIDE:
        return np.ones(k)
    levels = np.array([10, -10, 5, -5, 0])
    if k % 512:
        return np.exp2(np.random.permutation(np.resize(levels, k // 32))).repeat(32)
    a = np.empty((k // 512, 16))
    for p in range(k // 512):
        a[p, :8] = np.random.permutation(np.resize(levels, 8))
        for g in range(8):
            far = levels[np.abs(levels - a[p, g]) >= 10]
            a[p, g + 8] = far[np.random.randint(len(far))]
    return np.exp2(a.ravel()).repeat(32)


BF16 = ml_dtypes.bfloat16


def bf(x):
    return np.asarray(x, np.float32).astype(BF16)


def f64(x):
    return np.asarray(x).astype(np.float64)


E2M1 = np.array([0.0, 0.5, 1.0, 1.5, 2.0, 3.0, 4.0, 6.0, -0.0, -0.5, -1.0, -1.5, -2.0, -3.0, -4.0, -6.0])


def pack_weight(w, fmt):
    k, n = w.shape
    w = f64(bf(w)).reshape(k // 32, 32, n)
    amax = np.abs(w).max(1)
    if fmt == "e4m3":
        byte = np.frexp(amax)[1] - 1 + 127 - 7
    else:
        mant, ex = np.frexp(amax / 6.0)
        byte = np.where(mant > 0.5, ex, ex - 1) + 127
    byte = np.clip(np.where(amax > 0, byte, 1), 1, 254)
    scaled = (w * np.exp2(127.0 - byte)[:, None, :]).reshape(k, n).astype(np.float32)
    by_word = np.ascontiguousarray(scaled.reshape(k // 512, 128, 4, n).transpose(0, 1, 3, 2))
    if fmt == "e4m3":
        words = by_word.astype(ml_dtypes.float8_e4m3fn).view(np.uint8)
    else:
        c = by_word.astype(ml_dtypes.float4_e2m1fn).view(np.uint8) & 0xF
        words = c[..., 0::2] | (c[..., 1::2] << 4)
    return np.ascontiguousarray(words), np.ascontiguousarray(byte.astype(np.uint8).reshape(k // 512, 16, n))


def unpack_weight(words, scales, fmt):
    g, p, n, _ = words.shape
    if fmt == "e4m3":
        vals = np.ascontiguousarray(words).view(ml_dtypes.float8_e4m3fn).astype(np.float64)
    else:
        nib = np.empty((g, p, n, 4), np.uint8)
        nib[..., 0::2] = words & 0xF
        nib[..., 1::2] = words >> 4
        vals = E2M1[nib]
    vals = vals * np.repeat(np.exp2(scales.astype(np.float64) - 127.0), 8, axis=1)[..., None]
    return vals.transpose(0, 1, 3, 2).reshape(g * 512, n)
def pack4(w):
    words, scales = pack_weight(w, "e2m1")
    return words.reshape(words.shape[0], 128, -1), scales


def unpack4(words, scales):
    return unpack_weight(words.reshape(words.shape[0], 128, -1, 2), scales, "e2m1")


B, V, H = 2048, 1024, 512


def draw0():
    c = mx_kscale(H)
    t = mx_kscale(B)
    u = mx_kscale(B)
    v = bf(np.random.uniform(-1.0, 1.0, (B, V)) * u[:, None])
    hp = bf(np.random.uniform(-1.0, 1.0, (B, H)) / u[:, None])
    hf = bf(np.random.uniform(-1.0, 1.0, (B, H)) * c)
    hn = bf(np.random.uniform(-1.0, 1.0, (B, H)) / t[:, None])
    w = np.random.standard_normal((V, H)) * 2.0 / np.sqrt(H) / c
    w_words, w_scales = pack4(w.T)
    return {"v": v,
            "hp": hp,
            "hf": hf,
            "hn": hn,
            "w_words": w_words,
            "w_scales": w_scales,
            "b": bf(0.3 * np.random.standard_normal(V)),
            "s": bf((1.0 + 0.1 * np.random.standard_normal(B)) * t)}


def visible_mean_field(h, w_t, b):
    return np.tanh((mxq(h, 1, "e4m3") @ w_t) + b)


def correlation(vis, hid):
    return mxq(vis, 0, "e4m3").T @ mxq(hid, 0, "e4m3")


def core(v, hp, hf, hn, w_words, w_scales, b, s):
    n_rows = v.shape[0]
    v1 = visible_mean_field(f64(hf), unpack4(w_words, w_scales), f64(b))
    v1s = f64(s)[:, None] * v1
    neg = correlation(v1s, f64(hn))
    pos = correlation(f64(v), f64(hp))
    g = (pos - neg) / np.sqrt(n_rows)
    return g


def e4m3fn_bytes(y):
    return np.clip(np.asarray(y, np.float64), -448.0, 448.0).astype(np.float32).astype(ml_dtypes.float8_e4m3fn).view(np.uint8)


def e4m3fn_values(b):
    return np.asarray(b, np.uint8).view(ml_dtypes.float8_e4m3fn).astype(np.float64)


def setup_inputs():
    d = draw0()
    x0 = np.asarray(d['v']).astype(np.float64)
    s = (np.max(np.abs(x0), axis=(1,), keepdims=True) / 448.0).astype(np.float32)
    out = {}
    for k, v in d.items():
        if k == 'v':
            out['v_bytes'] = e4m3fn_bytes(x0 / s.astype(np.float64))
            out['v_scale'] = s
        else:
            out[k] = v
    return out


def reference(v_bytes, v_scale, hp, hf, hn, w_words, w_scales, b, s):
    return core(e4m3fn_values(v_bytes) * v_scale.astype(np.float64), hp, hf, hn, w_words, w_scales, b, s)

@@ -1,0 +1,354 @@
+from contextlib import ExitStack
+
+import concourse.mybir as mybir
+from concourse.masks import make_identity
+
+B, V, H = 2048, 1024, 512
+FLOPS = 3 * 2 * B * V * H
+
+F32 = mybir.dt.float32
+BF16 = mybir.dt.bfloat16
+U32 = mybir.dt.uint32
+I32 = mybir.dt.int32
+U8 = mybir.dt.uint8
+E4M3 = mybir.dt.float8_e4m3fn
+E4M3X4 = mybir.dt.float8_e4m3fn_x4
+E2M1X4 = mybir.dt.float4_e2m1fn_x4
+ACT = mybir.ActivationFunctionType
+ALU = mybir.AluOpType
+
+P = 128
+G = 4
+MT = V // P
+HALF = MT // 2
+
+
+def tile_persistentmeanfieldisingrbmgradient_w4_kernel(
+    tc, v_bytes, v_scale, hp, hf, hn, w_words, w_scales, b, s, out
+):
+    nc = tc.nc
+    with ExitStack() as ctx:
+        keep = ctx.enter_context(tc.tile_pool(name="keep", bufs=1))
+        ring = ctx.enter_context(tc.tile_pool(name="ring", bufs=4))
+        psum = ctx.enter_context(tc.psum_pool(name="psum", bufs=1))
+
+        def kt(name, shape, dtype):
+            return keep.tile(shape, dtype, name=name, align_bytes=256)
+
+        counts = {"f": 0, "t": 0}
+
+        def bank(kind, shape):
+            i = counts[kind] % 4
+            counts[kind] = counts[kind] + 1
+            nm = kind + str(i)
+            return psum.tile(shape, F32, name=nm, tag=nm)
+
+        def r4(nm):
+            return ring.tile([P, 4, 512], BF16, name=nm, tag="r4", bufs=6, align_bytes=256)
+
+        def grp(nm):
+            return ring.tile([P, 2048], BF16, name=nm, tag="grp", bufs=3, align_bytes=256)
+
+        hf_raw = [r4("hf_raw%d" % g) for g in range(G)]
+        hn_raw = [kt("hn_raw%d" % g, [P, 4, H], BF16) for g in range(G)]
+        hp_raw = [kt("hp_raw%d" % g, [P, 4, H], BF16) for g in range(G)]
+        v_raw = [kt("v_raw%d" % g, [P, 4, V], U8) for g in range(G)]
+        hf_codes = [kt("hf_codes%d" % g, [P, 512], U32) for g in range(G)]
+        hf_sc = [kt("hf_sc%d" % g, [P, 512], U8) for g in range(G)]
+        hn_codes = [kt("hn_codes%d" % g, [P, H], U32) for g in range(G)]
+        hn_sc = [kt("hn_sc%d" % g, [P, H], U8) for g in range(G)]
+        hp_codes = [kt("hp_codes%d" % g, [P, H], U32) for g in range(G)]
+        hp_sc = [kt("hp_sc%d" % g, [P, H], U8) for g in range(G)]
+        v1_codes = [[kt("v1_codes%d_%d" % (h, g), [P, 512], U32) for g in range(G)] for h in range(2)]
+        v1_sc = [[kt("v1_sc%d_%d" % (h, g), [P, 512], U8) for g in range(G)] for h in range(2)]
+        v_codes = [[kt("v_codes%d_%d" % (h, g), [P, 512], U32) for g in range(G)] for h in range(2)]
+        v_sc = [[kt("v_sc%d_%d" % (h, g), [P, 512], U8) for g in range(G)] for h in range(2)]
+        w_codes = kt("w_codes", [P, 2 * V], U8)
+        w_sc = kt("w_sc", [P, V], U8)
+        ident = kt("ident", [P, P], F32)
+        b_rows = kt("b_rows", [P, P], BF16)
+        b_rows32 = kt("b_rows32", [P, P], F32)
+        bias = kt("bias", [P, MT], F32)
+        s_bf = kt("s_bf", [P, G, 4], BF16)
+        s_neg = kt("s_neg", [P, G, 4], F32)
+        vs = kt("vs", [P, G, 4], F32)
+        warm = kt("warm", [P, 1], F32)
+
+        with tc.manual_schedule():
+            nc.vector.memset(w_sc[:].bitcast(I32), 0)
+            nc.vector.memset(b_rows[:], 0.0)
+            nc.vector.memset(warm[:], 0.0)
+            make_identity(nc, ident[:])
+            nc.scalar.dma_start(out=b_rows[0:MT, :], in_=b.rearrange("(m c) -> m c", c=P))
+            nc.scalar.dma_start(out=s_bf[:], in_=s.rearrange("(g p t) -> p g t", p=P, t=4))
+            nc.scalar.dma_start(out=vs[:], in_=v_scale.rearrange("(g p t) o -> p g (t o)", p=P, t=4))
+            nc.scalar.activation(warm[:], warm[:], ACT.Tanh)
+
+            def rows(x, g):
+                return x.rearrange("(g p t) k -> g p t k", p=P, t=4)[g]
+
+            nc.sync.dma_start(out=hf_raw[0][:, 0:2, :], in_=rows(hf, 0)[:, 0:2, :])
+            nc.sync.dma_start(out=hf_raw[0][:, 2:4, :], in_=rows(hf, 0)[:, 2:4, :])
+            for q in range(4):
+                nc.sync.dma_start(
+                    out=w_sc[32 * q : 32 * q + 4, :].bitcast(I32),
+                    in_=w_scales[0][4 * q : 4 * q + 4, :].bitcast(I32),
+                )
+            nc.sync.dma_start(out=w_codes[:], in_=w_words[0])
+            for g in range(1, G):
+                nc.sync.dma_start(out=hf_raw[g][:], in_=rows(hf, g))
+            for g in range(G):
+                nc.sync.dma_start(out=hn_raw[g][:], in_=rows(hn, g))
+            for g in range(G):
+                nc.sync.dma_start(out=v_raw[g][:], in_=rows(v_bytes, g))
+            for g in range(G):
+                nc.sync.dma_start(out=hp_raw[g][:], in_=rows(hp, g))
+
+            hf_grp = {}
+
+            tr_bank = {}
+
+            def hf_turn(g, h):
+                if h == 0:
+                    hf_grp[g] = grp("hf_grp%d" % g)
+                bk = bank("t", [P, 2, 2, P])
+                tr_bank[(g, h)] = bk
+                words = hf_raw[g][:].rearrange("p t k -> p (t k)").bitcast(F32)
+                for i in range(2):
+                    for u in range(2):
+                        base = 256 * (2 * h + i)
+                        nc.tensor.transpose(bk[:, i, u, :], words[:, base + u : base + 256 : 2], ident[:])
+
+            def hf_out(g, h):
+                dst = hf_grp[g][:, 1024 * h : 1024 * h + 1024].bitcast(F32).rearrange(
+                    "p (i m u) -> p i m u", i=2, u=2
+                )
+                src = tr_bank[(g, h)][:].rearrange("p i u m -> p i m u")
+                if h == 0:
+                    nc.vector.tensor_copy(out=dst, in_=src)
+                else:
+                    nc.scalar.copy(out=dst, in_=src)
+
+            def hf_quant(g, h):
+                nc.vector.quantize_mx(
+                    out=hf_codes[g][:, 256 * h : 256 * h + 256].bitcast(E4M3X4),
+                    scales=hf_sc[g][:, 256 * h : 256 * h + 256],
+                    in_=hf_grp[g][:, 1024 * h : 1024 * h + 1024],
+                )
+
+            f_bank = {}
+            th = {}
+            t_bank = {}
+            v1_grp = {}
+
+            def field(u):
+                g, m = u // MT, u % MT
+                f_bank[u] = bank("f", [P, 512])
+                nc.tensor.matmul_mx(
+                    out=f_bank[u][:],
+                    lhsT=w_codes[:, 256 * m : 256 * m + 256].bitcast(E2M1X4),
+                    lhsT_scale=w_sc[:, P * m : P * m + P],
+                    rhs=hf_codes[g][:].bitcast(E4M3X4),
+                    rhs_scale=hf_sc[g][:],
+                    start=True,
+                    stop=True,
+                )
+
+            def tanh(u):
+                m = u % MT
+                th[u] = ring.tile([P, 4, P], F32, name="th%d" % u, tag="th", bufs=6)
+                nc.scalar.activation(
+                    th[u][:].rearrange("p t q -> p (t q)"), f_bank[u][:], ACT.Tanh, bias=bias[:, m : m + 1]
+                )
+
+            def turn(u):
+                t_bank[u] = bank("t", [P, 4, P])
+                for t in range(4):
+                    nc.tensor.transpose(t_bank[u][:, t, :], th[u][:, t, :], ident[:])
+
+            def weight(u):
+                g, m = u // MT, u % MT
+                h, mm = m // HALF, m % HALF
+                if mm == 0:
+                    v1_grp[(h, g)] = ring.tile(
+                        [P, 2048], BF16, name="v1_grp%d_%d" % (h, g), tag="v1_grp", bufs=4, align_bytes=256
+                    )
+                nc.vector.tensor_tensor(
+                    out=v1_grp[(h, g)][:, 512 * mm : 512 * mm + 512].rearrange("p (q t) -> p q t", t=4),
+                    in0=t_bank[u][:].rearrange("p t q -> p q t"),
+                    in1=s_neg[:, g, :].unsqueeze(1).to_broadcast([P, P, 4]),
+                    op=ALU.mult,
+                )
+
+            def v1_quant(h, g):
+                nc.vector.quantize_mx(
+                    out=v1_codes[h][g][:].bitcast(E4M3X4), scales=v1_sc[h][g][:], in_=v1_grp[(h, g)][:]
+                )
+
+            h_grp = {}
+
+            def h_new(nm, g):
+                h_grp[(nm, g)] = ring.tile(
+                    [P, 2048], BF16, name="h_grp_%s%d" % (nm, g), tag="h_grp", bufs=6, align_bytes=256
+                )
+
+            def h_mix_gp(nm, raw, g, c0, n):
+                nc.gpsimd.tensor_scalar(
+                    out=h_grp[(nm, g)][:, 4 * c0 : 4 * (c0 + n)].rearrange("p (c t) -> p c t", t=4),
+                    in0=raw[g][:, :, c0 : c0 + n].rearrange("p t c -> p c t"),
+                    scalar1=1.0,
+                    scalar2=0.0,
+                    op0=ALU.mult,
+                    op1=ALU.add,
+                )
+
+            def mix_views(dst, src):
+                return (
+                    dst.rearrange("p (c i t) -> p c t i", i=4, t=4),
+                    src.rearrange("p t (c i) -> p c t i", i=4),
+                )
+
+            def h_mix_v(nm, raw, g):
+                d, sr = mix_views(h_grp[(nm, g)][:], raw[g][:])
+                nc.vector.tensor_copy(out=d, in_=sr)
+
+            def h_quant(nm, codes, sc, g):
+                nc.vector.quantize_mx(out=codes[g][:].bitcast(E4M3X4), scales=sc[g][:], in_=h_grp[(nm, g)][:])
+
+            v_wide = {}
+            v_grp = {}
+
+            def widen(h, g, t):
+                if t == 0:
+                    v_wide[(h, g)] = r4("v_wide%d_%d" % (h, g))
+                nc.scalar.activation(
+                    v_wide[(h, g)][:, t, :],
+                    v_raw[g][:, t, 512 * h : 512 * h + 512].bitcast(E4M3),
+                    ACT.Copy,
+                    scale=vs[:, g, t : t + 1],
+                )
+
+            def v_mix(h, g):
+                v_grp[(h, g)] = grp("v_grp%d_%d" % (h, g))
+                d, sr = mix_views(v_grp[(h, g)][:], v_wide[(h, g)][:])
+                nc.vector.tensor_copy(out=d, in_=sr)
+
+            def v_quant(h, g):
+                nc.vector.quantize_mx(
+                    out=v_codes[h][g][:].bitcast(E4M3X4), scales=v_sc[h][g][:], in_=v_grp[(h, g)][:]
+                )
+
+            nc.vector.tensor_scalar(
+                out=s_neg[:], in0=s_bf[:], scalar1=-1.0, scalar2=None, op0=ALU.mult
+            )
+            nc.vector.tensor_copy(out=b_rows32[:], in_=b_rows[:])
+            hf_turn(0, 0)
+            hf_turn(0, 1)
+            b_bank = bank("t", [P, P])
+            nc.tensor.transpose(b_bank[:], b_rows32[:], ident[:])
+            hf_out(0, 0)
+            hf_out(0, 1)
+            nc.vector.tensor_copy(out=bias[:], in_=b_bank[:, 0:MT])
+            hf_quant(0, 0)
+            hf_quant(0, 1)
+            hf_turn(1, 0)
+            hf_turn(1, 1)
+            hf_out(1, 0)
+            hf_out(1, 1)
+            for u in range(4):
+                field(u)
+            hf_quant(1, 0)
+            hf_quant(1, 1)
+            tanh(0)
+            tanh(1)
+
+            widen_list = [(h, g, t) for h in range(2) for g in range(G) for t in range(4)]
+            gp_list = []
+            for g in range(G):
+                gp_list = gp_list + [("n", hn_raw, g, c) for c in range(4)]
+            for g in range(2):
+                gp_list = gp_list + [("p", hp_raw, g, c) for c in range(4)]
+            for (nm, raw, g, c) in gp_list:
+                if c == 0:
+                    h_new(nm, g)
+                h_mix_gp(nm, raw, g, 128 * c, 128)
+
+            npairs = G * MT // 2
+            nw = 0
+            for j in range(npairs):
+                if j == 0:
+                    hf_turn(2, 0)
+                    hf_turn(2, 1)
+                    hf_out(2, 0)
+                    hf_out(2, 1)
+                if j == 1:
+                    hf_turn(3, 0)
+                    hf_turn(3, 1)
+                    hf_out(3, 0)
+                    hf_out(3, 1)
+                turn(2 * j)
+                turn(2 * j + 1)
+                if j + 2 < npairs:
+                    field(2 * j + 4)
+                    field(2 * j + 5)
+                if j + 1 < npairs:
+                    tanh(2 * j + 2)
+                    tanh(2 * j + 3)
+                weight(2 * j)
+                if j < 2:
+                    hf_quant(2 + j, 0)
+                    hf_quant(2 + j, 1)
+                weight(2 * j + 1)
+                if j % 2 == 0 and j > 0:
+                    k = j // 2 - 1
+                    v1_quant(k % 2, k // 2)
+                if j >= 5 and nw < len(widen_list):
+                    widen(*widen_list[nw])
+                    nw = nw + 1
+            v1_quant(1, G - 1)
+
+            while nw < 8:
+                widen(*widen_list[nw])
+                nw = nw + 1
+            for h in range(2):
+                kind = "f" if h == 0 else "t"
+                acc = [bank(kind, [P, H]) for m in range(HALF)]
+
+                def passes(codes, sc, rc, rs, g, first, last):
+                    for mm in range(HALF):
+                        nc.tensor.matmul_mx(
+                            out=acc[mm][:],
+                            lhsT=codes[:, P * mm : P * mm + P].bitcast(E4M3X4),
+                            lhsT_scale=sc[:, P * mm : P * mm + P],
+                            rhs=rc[g][:].bitcast(E4M3X4),
+                            rhs_scale=rs[g][:],
+                            start=first,
+                            stop=last,
+                        )
+
+                for g in range(G):
+                    if h == 0:
+                        h_quant("n", hn_codes, hn_sc, g)
+                    v_mix(h, g)
+                    if h == 0:
+                        if g >= 2:
+                            h_new("p", g)
+                            h_mix_v("p", hp_raw, g)
+                        h_quant("p", hp_codes, hp_sc, g)
+                    v_quant(h, g)
+                    for i in range(4):
+                        if nw < len(widen_list):
+                            widen(*widen_list[nw])
+                            nw = nw + 1
+                    passes(v1_codes[h][g], v1_sc[h][g], hn_codes, hn_sc, g, g == 0, False)
+                    passes(v_codes[h][g], v_sc[h][g], hp_codes, hp_sc, g, False, g == G - 1)
+                for mm in range(HALF):
+                    m = HALF * h + mm
+                    res = ring.tile([P, H], F32, name="res%d" % m, tag="res", bufs=4)
+                    if mm % 2 == 1 or h == 0:
+                        nc.scalar.activation(res[:], acc[mm][:], ACT.Copy, scale=float(B) ** -0.5)
+                    else:
+                        nc.vector.tensor_scalar(
+                            out=res[:], in0=acc[mm][:], scalar1=float(B) ** -0.5, scalar2=None, op0=ALU.mult
+                        )
+                    nc.sync.dma_start(out=out[P * m : P * m + P, :], in_=res[:])

@@ -21,6 +21,14 @@ P = 128
 G = 4
 MT = V // P
 HALF = MT // 2
+S_SHARE = ((2, 1), (2, 2), (2, 3), (3, 0), (3, 1), (3, 2))
+G_SHARE = ((0, 2), (0, 3))
+V_OUT = (6,)
+STORE_AT = ((0, 14), (1, 14), (2, 15), (3, 15), (4, 15), (5, 15), (6, 15), (7, 15))
+WIDEN_PER_JOB = 3
+GP_COLS = 128
+HQ_AT = (7, 10, 11)
+WIDEN_AT = {}
 
 
 def tile_persistentmeanfieldisingrbmgradient_w4_kernel(
@@ -44,14 +52,14 @@ def tile_persistentmeanfieldisingrbmgradient_w4_kernel(
             return psum.tile(shape, F32, name=nm, tag=nm)
 
         def r4(nm):
-            return ring.tile([P, 4, 512], BF16, name=nm, tag="r4", bufs=6, align_bytes=256)
+            return ring.tile([P, 4, 512], BF16, name=nm, tag="r4", bufs=12, align_bytes=256)
 
         def grp(nm):
-            return ring.tile([P, 2048], BF16, name=nm, tag="grp", bufs=3, align_bytes=256)
+            return ring.tile([P, 2048], BF16, name=nm, tag="grp", bufs=2, align_bytes=256)
 
         hf_raw = [r4("hf_raw%d" % g) for g in range(G)]
-        hn_raw = [kt("hn_raw%d" % g, [P, 4, H], BF16) for g in range(G)]
-        hp_raw = [kt("hp_raw%d" % g, [P, 4, H], BF16) for g in range(G)]
+        hn_raw = [r4("hn_raw%d" % g) for g in range(G)]
+        hp_raw = [r4("hp_raw%d" % g) for g in range(G)]
         v_raw = [kt("v_raw%d" % g, [P, 4, V], U8) for g in range(G)]
         hf_codes = [kt("hf_codes%d" % g, [P, 512], U32) for g in range(G)]
         hf_sc = [kt("hf_sc%d" % g, [P, 512], U8) for g in range(G)]
@@ -81,7 +89,7 @@ def tile_persistentmeanfieldisingrbmgradient_w4_kernel(
             make_identity(nc, ident[:])
             nc.scalar.dma_start(out=b_rows[0:MT, :], in_=b.rearrange("(m c) -> m c", c=P))
             nc.scalar.dma_start(out=s_bf[:], in_=s.rearrange("(g p t) -> p g t", p=P, t=4))
-            nc.scalar.dma_start(out=vs[:], in_=v_scale.rearrange("(g p t) o -> p g (t o)", p=P, t=4))
+            nc.gpsimd.dma_start(out=vs[:], in_=v_scale.rearrange("(g p t) o -> p g (t o)", p=P, t=4))
             nc.scalar.activation(warm[:], warm[:], ACT.Tanh)
 
             def rows(x, g):
@@ -89,20 +97,18 @@ def tile_persistentmeanfieldisingrbmgradient_w4_kernel(
 
             nc.sync.dma_start(out=hf_raw[0][:, 0:2, :], in_=rows(hf, 0)[:, 0:2, :])
             nc.sync.dma_start(out=hf_raw[0][:, 2:4, :], in_=rows(hf, 0)[:, 2:4, :])
+            nc.sync.dma_start(out=w_codes[:], in_=w_words[0])
             for q in range(4):
                 nc.sync.dma_start(
                     out=w_sc[32 * q : 32 * q + 4, :].bitcast(I32),
                     in_=w_scales[0][4 * q : 4 * q + 4, :].bitcast(I32),
                 )
-            nc.sync.dma_start(out=w_codes[:], in_=w_words[0])
-            for g in range(1, G):
-                nc.sync.dma_start(out=hf_raw[g][:], in_=rows(hf, g))
-            for g in range(G):
-                nc.sync.dma_start(out=hn_raw[g][:], in_=rows(hn, g))
-            for g in range(G):
-                nc.sync.dma_start(out=v_raw[g][:], in_=rows(v_bytes, g))
-            for g in range(G):
-                nc.sync.dma_start(out=hp_raw[g][:], in_=rows(hp, g))
+            for (dst, x, g) in (
+                (hf_raw, hf, 1), (hn_raw, hn, 0), (hf_raw, hf, 2), (v_raw, v_bytes, 0), (hf_raw, hf, 3),
+                (hn_raw, hn, 1), (hn_raw, hn, 2), (v_raw, v_bytes, 1), (hp_raw, hp, 0), (hn_raw, hn, 3), (v_raw, v_bytes, 2),
+                (hp_raw, hp, 1), (v_raw, v_bytes, 3), (hp_raw, hp, 3), (hp_raw, hp, 2),
+            ):
+                nc.sync.dma_start(out=dst[g][:], in_=rows(x, g))
 
             hf_grp = {}
 
@@ -156,7 +162,7 @@ def tile_persistentmeanfieldisingrbmgradient_w4_kernel(
 
             def tanh(u):
                 m = u % MT
-                th[u] = ring.tile([P, 4, P], F32, name="th%d" % u, tag="th", bufs=6)
+                th[u] = ring.tile([P, 4, P], F32, name="th%d" % u, tag="th", bufs=8)
                 nc.scalar.activation(
                     th[u][:].rearrange("p t q -> p (t q)"), f_bank[u][:], ACT.Tanh, bias=bias[:, m : m + 1]
                 )
@@ -228,64 +234,96 @@ def tile_persistentmeanfieldisingrbmgradient_w4_kernel(
                     scale=vs[:, g, t : t + 1],
                 )
 
-            def v_mix(h, g):
-                v_grp[(h, g)] = grp("v_grp%d_%d" % (h, g))
-                d, sr = mix_views(v_grp[(h, g)][:], v_wide[(h, g)][:])
-                nc.vector.tensor_copy(out=d, in_=sr)
+            def v_mix(mp, g, c):
+                if c == 0:
+                    v_grp[(mp, g)] = ring.tile(
+                        [P, 1024], BF16, name="v_grp%d_%d" % (mp, g), tag="v_grp", bufs=5, align_bytes=256
+                    )
+                c0 = P * (2 * (mp % 2) + c)
+                dst = v_grp[(mp, g)][:, 512 * c : 512 * c + 512]
+                src = v_wide[(mp // 2, g)][:, :, c0 : c0 + P]
+                d, sr = mix_views(dst, src)
+                if c == 1 and (mp, g) in S_SHARE:
+                    nc.scalar.copy(out=d, in_=sr)
+                elif (mp, g) in G_SHARE:
+                    nc.gpsimd.tensor_scalar(
+                        out=dst.rearrange("p (c t) -> p c t", t=4),
+                        in0=src.rearrange("p t c -> p c t"),
+                        scalar1=1.0,
+                        scalar2=0.0,
+                        op0=ALU.mult,
+                        op1=ALU.add,
+                    )
+                else:
+                    nc.vector.tensor_copy(out=d, in_=sr)
 
-            def v_quant(h, g):
+            def v_quant(mp, g):
+                c0 = 256 * (mp % 2)
                 nc.vector.quantize_mx(
-                    out=v_codes[h][g][:].bitcast(E4M3X4), scales=v_sc[h][g][:], in_=v_grp[(h, g)][:]
+                    out=v_codes[mp // 2][g][:, c0 : c0 + 256].bitcast(E4M3X4),
+                    scales=v_sc[mp // 2][g][:, c0 : c0 + 256],
+                    in_=v_grp[(mp, g)][:],
                 )
 
+            def h_mix_s(nm, raw, g):
+                h_new(nm, g)
+                d, sr = mix_views(h_grp[(nm, g)][:], raw[g][:])
+                nc.scalar.copy(out=d, in_=sr)
+
+            def quant_hn(g):
+                h_quant("n", hn_codes, hn_sc, g)
+
+            def quant_hp(g):
+                h_quant("p", hp_codes, hp_sc, g)
+
+            def mix_gp(nm, raw, g):
+                h_new(nm, g)
+                for c in range(H // GP_COLS):
+                    h_mix_gp(nm, raw, g, GP_COLS * c, GP_COLS)
+
+            mix_gp("n", hn_raw, 0)
+            mix_gp("n", hn_raw, 1)
+            mix_gp("n", hn_raw, 2)
+            mix_gp("n", hn_raw, 3)
+
+            hf_turn(0, 0)
+            hf_turn(0, 1)
+            hf_out(0, 0)
+            hf_out(0, 1)
+            nc.vector.tensor_copy(out=b_rows32[:], in_=b_rows[:])
+            hf_quant(0, 0)
+            b_bank = bank("t", [P, P])
+            nc.tensor.transpose(b_bank[:], b_rows32[:], ident[:])
+            nc.vector.tensor_copy(out=bias[:], in_=b_bank[:, 0:MT])
+            hf_quant(0, 1)
             nc.vector.tensor_scalar(
                 out=s_neg[:], in0=s_bf[:], scalar1=-1.0, scalar2=None, op0=ALU.mult
             )
-            nc.vector.tensor_copy(out=b_rows32[:], in_=b_rows[:])
-            hf_turn(0, 0)
-            hf_turn(0, 1)
-            b_bank = bank("t", [P, P])
-            nc.tensor.transpose(b_bank[:], b_rows32[:], ident[:])
-            hf_out(0, 0)
-            hf_out(0, 1)
-            nc.vector.tensor_copy(out=bias[:], in_=b_bank[:, 0:MT])
-            hf_quant(0, 0)
-            hf_quant(0, 1)
             hf_turn(1, 0)
             hf_turn(1, 1)
             hf_out(1, 0)
             hf_out(1, 1)
             for u in range(4):
                 field(u)
-            hf_quant(1, 0)
-            hf_quant(1, 1)
             tanh(0)
             tanh(1)
+            hf_quant(1, 0)
+            hf_quant(1, 1)
+            mix_gp("p", hp_raw, 0)
+            mix_gp("p", hp_raw, 1)
 
             widen_list = [(h, g, t) for h in range(2) for g in range(G) for t in range(4)]
-            gp_list = []
-            for g in range(G):
-                gp_list = gp_list + [("n", hn_raw, g, c) for c in range(4)]
-            for g in range(2):
-                gp_list = gp_list + [("p", hp_raw, g, c) for c in range(4)]
-            for (nm, raw, g, c) in gp_list:
-                if c == 0:
-                    h_new(nm, g)
-                h_mix_gp(nm, raw, g, 128 * c, 128)
-
-            npairs = G * MT // 2
+            hq = [(quant_hn, 0), (quant_hn, 1), (quant_hn, 2), (quant_hn, 3), (quant_hp, 0), (quant_hp, 1), (quant_hp, 2), (quant_hp, 3)]
+            nq = 0
             nw = 0
+            npairs = G * MT // 2
             for j in range(npairs):
-                if j == 0:
-                    hf_turn(2, 0)
-                    hf_turn(2, 1)
-                    hf_out(2, 0)
-                    hf_out(2, 1)
-                if j == 1:
-                    hf_turn(3, 0)
-                    hf_turn(3, 1)
-                    hf_out(3, 0)
-                    hf_out(3, 1)
+                if j < 2:
+                    hf_turn(2 + j, 0)
+                    hf_turn(2 + j, 1)
+                    hf_out(2 + j, 0)
+                    hf_out(2 + j, 1)
+                    hf_quant(2 + j, 0)
                 turn(2 * j)
                 turn(2 * j + 1)
                 if j + 2 < npairs:
@@ -296,59 +334,73 @@ def tile_persistentmeanfieldisingrbmgradient_w4_kernel(
                     tanh(2 * j + 3)
                 weight(2 * j)
                 if j < 2:
-                    hf_quant(2 + j, 0)
                     hf_quant(2 + j, 1)
-                weight(2 * j + 1)
                 if j % 2 == 0 and j > 0:
                     k = j // 2 - 1
                     v1_quant(k % 2, k // 2)
-                if j >= 5 and nw < len(widen_list):
+                weight(2 * j + 1)
+                if j in HQ_AT:
+                    hq[nq][0](hq[nq][1])
+                    nq = nq + 1
+                for k in range(WIDEN_AT.get(j, 1)):
                     widen(*widen_list[nw])
                     nw = nw + 1
+            mix_gp("p", hp_raw, 3)
             v1_quant(1, G - 1)
 
-            while nw < 8:
-                widen(*widen_list[nw])
-                nw = nw + 1
-            for h in range(2):
-                kind = "f" if h == 0 else "t"
-                acc = [bank(kind, [P, H]) for m in range(HALF)]
+            acc = [bank("f", [P, H]) for m in range(HALF)] + [bank("t", [P, H]) for m in range(HALF)]
 
-                def passes(codes, sc, rc, rs, g, first, last):
+            def one_pass(m, codes, sc, rc, rs, g, first, last):
+                c0 = P * (m % HALF)
+                nc.tensor.matmul_mx(
+                    out=acc[m][:],
+                    lhsT=codes[m // HALF][g][:, c0 : c0 + P].bitcast(E4M3X4),
+                    lhsT_scale=sc[m // HALF][g][:, c0 : c0 + P],
+                    rhs=rc[g][:].bitcast(E4M3X4),
+                    rhs_scale=rs[g][:],
+                    start=first,
+                    stop=last,
+                )
+
+            def store(m):
+                res = ring.tile([P, H], F32, name="res%d" % m, tag="th", bufs=8)
+                if m in V_OUT:
+                    nc.vector.tensor_scalar(
+                        out=res[:], in0=acc[m][:], scalar1=float(B) ** -0.5, scalar2=None, op0=ALU.mult
+                    )
+                else:
+                    nc.scalar.activation(res[:], acc[m][:], ACT.Copy, scale=float(B) ** -0.5)
+                nc.sync.dma_start(out=out[P * m : P * m + P, :], in_=res[:])
+
+            while nq < 4:
+                hq[nq][0](hq[nq][1])
+                nq = nq + 1
+            for g in range(G):
+                for h in range(2):
                     for mm in range(HALF):
-                        nc.tensor.matmul_mx(
-                            out=acc[mm][:],
-                            lhsT=codes[:, P * mm : P * mm + P].bitcast(E4M3X4),
-                            lhsT_scale=sc[:, P * mm : P * mm + P],
-                            rhs=rc[g][:].bitcast(E4M3X4),
-                            rhs_scale=rs[g][:],
-                            start=first,
-                            stop=last,
-                        )
+                        one_pass(HALF * h + mm, v1_codes, v1_sc, hn_codes, hn_sc, g, g == 0, False)
+            h_mix_s("p", hp_raw, 2)
+            jobs = [(mp, g) for mp in range(4) for g in range(G)]
 
-                for g in range(G):
-                    if h == 0:
-                        h_quant("n", hn_codes, hn_sc, g)
-                    v_mix(h, g)
-                    if h == 0:
-                        if g >= 2:
-                            h_new("p", g)
-                            h_mix_v("p", hp_raw, g)
-                        h_quant("p", hp_codes, hp_sc, g)
-                    v_quant(h, g)
-                    for i in range(4):
-                        if nw < len(widen_list):
-                            widen(*widen_list[nw])
-                            nw = nw + 1
-                    passes(v1_codes[h][g], v1_sc[h][g], hn_codes, hn_sc, g, g == 0, False)
-                    passes(v_codes[h][g], v_sc[h][g], hp_codes, hp_sc, g, False, g == G - 1)
-                for mm in range(HALF):
-                    m = HALF * h + mm
-                    res = ring.tile([P, H], F32, name="res%d" % m, tag="res", bufs=4)
-                    if mm % 2 == 1 or h == 0:
-                        nc.scalar.activation(res[:], acc[mm][:], ACT.Copy, scale=float(B) ** -0.5)
-                    else:
-                        nc.vector.tensor_scalar(
-                            out=res[:], in0=acc[mm][:], scalar1=float(B) ** -0.5, scalar2=None, op0=ALU.mult
-                        )
-                    nc.sync.dma_start(out=out[P * m : P * m + P, :], in_=res[:])
+            def mix_job(i):
+                for c in range(2):
+                    v_mix(jobs[i][0], jobs[i][1], c)
+
+            mix_job(0)
+            for i in range(len(jobs)):
+                for k in range(WIDEN_PER_JOB):
+                    if nw < len(widen_list):
+                        widen(*widen_list[nw])
+                        nw = nw + 1
+                if i + 1 < len(jobs):
+                    mix_job(i + 1)
+                v_quant(*jobs[i])
+                if nq < len(hq):
+                    hq[nq][0](hq[nq][1])
+                    nq = nq + 1
+                mp, g = jobs[i]
+                for c in range(2):
+                    one_pass(2 * mp + c, v_codes, v_sc, hp_codes, hp_sc, g, False, g == G - 1)
+                for (m, at) in STORE_AT:
+                    if at == i:
+                        store(m)

@@ -22,13 +22,21 @@ G = 4
 MT = V // P
 HALF = MT // 2
 S_SHARE = ((2, 1), (2, 2), (2, 3), (3, 0), (3, 1), (3, 2))
-G_SHARE = ((0, 2), (0, 3))
-V_OUT = (6,)
-STORE_AT = ((0, 14), (1, 14), (2, 15), (3, 15), (4, 15), (5, 15), (6, 15), (7, 15))
-WIDEN_PER_JOB = 3
+G_SHARE = ((0, 3),)
+V_OUT = (5, 6)
+STORE_AT = ((0, 13), (1, 13), (2, 14), (3, 14), (4, 15), (5, 15), (6, 15), (7, 15))
+WIDEN_PER_JOB = 4
 GP_COLS = 128
-HQ_AT = (7, 10, 11)
+V1Q = 4
+GP_LATE = (3,)
+S_HP = (2,)
+V_HP = ()
+V_N0 = 0
+HQ_AT = (2, 7, 14)
 WIDEN_AT = {}
+TR_AT = {1: 1, 4: 2, 8: 3}
+HEAD_WIDEN = (0, 0, 0)
+LOADS = ('hf0a', 'hf0b', 'w', 'wsc', 'hn0', 'hf1', 'v0', 'hn1', 'hn3', 'v1', 'hf2', 'hn2', 'hp2', 'v2', 'hp3', 'hp0', 'hf3', 'hp1', 'v3')
 
 
 def tile_persistentmeanfieldisingrbmgradient_w4_kernel(
@@ -67,10 +75,10 @@ def tile_persistentmeanfieldisingrbmgradient_w4_kernel(
         hn_sc = [kt("hn_sc%d" % g, [P, H], U8) for g in range(G)]
         hp_codes = [kt("hp_codes%d" % g, [P, H], U32) for g in range(G)]
         hp_sc = [kt("hp_sc%d" % g, [P, H], U8) for g in range(G)]
-        v1_codes = [[kt("v1_codes%d_%d" % (h, g), [P, 512], U32) for g in range(G)] for h in range(2)]
-        v1_sc = [[kt("v1_sc%d_%d" % (h, g), [P, 512], U8) for g in range(G)] for h in range(2)]
-        v_codes = [[kt("v_codes%d_%d" % (h, g), [P, 512], U32) for g in range(G)] for h in range(2)]
-        v_sc = [[kt("v_sc%d_%d" % (h, g), [P, 512], U8) for g in range(G)] for h in range(2)]
+        v1_codes = [kt("v1_codes%d" % g, [P, V], U32) for g in range(G)]
+        v1_sc = [kt("v1_sc%d" % g, [P, V], U8) for g in range(G)]
+        v_codes = [kt("v_codes%d" % g, [P, V], U32) for g in range(G)]
+        v_sc = [kt("v_sc%d" % g, [P, V], U8) for g in range(G)]
         w_codes = kt("w_codes", [P, 2 * V], U8)
         w_sc = kt("w_sc", [P, V], U8)
         ident = kt("ident", [P, P], F32)
@@ -83,8 +91,8 @@ def tile_persistentmeanfieldisingrbmgradient_w4_kernel(
         warm = kt("warm", [P, 1], F32)
 
         with tc.manual_schedule():
-            nc.vector.memset(w_sc[:].bitcast(I32), 0)
             nc.vector.memset(b_rows[:], 0.0)
+            nc.vector.memset(w_sc[:].bitcast(I32), 0)
             nc.vector.memset(warm[:], 0.0)
             make_identity(nc, ident[:])
             nc.scalar.dma_start(out=b_rows[0:MT, :], in_=b.rearrange("(m c) -> m c", c=P))
@@ -95,20 +103,23 @@ def tile_persistentmeanfieldisingrbmgradient_w4_kernel(
             def rows(x, g):
                 return x.rearrange("(g p t) k -> g p t k", p=P, t=4)[g]
 
-            nc.sync.dma_start(out=hf_raw[0][:, 0:2, :], in_=rows(hf, 0)[:, 0:2, :])
-            nc.sync.dma_start(out=hf_raw[0][:, 2:4, :], in_=rows(hf, 0)[:, 2:4, :])
-            nc.sync.dma_start(out=w_codes[:], in_=w_words[0])
-            for q in range(4):
-                nc.sync.dma_start(
-                    out=w_sc[32 * q : 32 * q + 4, :].bitcast(I32),
-                    in_=w_scales[0][4 * q : 4 * q + 4, :].bitcast(I32),
-                )
-            for (dst, x, g) in (
-                (hf_raw, hf, 1), (hn_raw, hn, 0), (hf_raw, hf, 2), (v_raw, v_bytes, 0), (hf_raw, hf, 3),
-                (hn_raw, hn, 1), (hn_raw, hn, 2), (v_raw, v_bytes, 1), (hp_raw, hp, 0), (hn_raw, hn, 3), (v_raw, v_bytes, 2),
-                (hp_raw, hp, 1), (v_raw, v_bytes, 3), (hp_raw, hp, 3), (hp_raw, hp, 2),
-            ):
-                nc.sync.dma_start(out=dst[g][:], in_=rows(x, g))
+            big = {"hf": (hf_raw, hf), "hn": (hn_raw, hn), "hp": (hp_raw, hp), "v": (v_raw, v_bytes)}
+            for nm in LOADS:
+                if nm == "hf0a":
+                    nc.sync.dma_start(out=hf_raw[0][:, 0:2, :], in_=rows(hf, 0)[:, 0:2, :])
+                elif nm == "hf0b":
+                    nc.sync.dma_start(out=hf_raw[0][:, 2:4, :], in_=rows(hf, 0)[:, 2:4, :])
+                elif nm == "w":
+                    nc.sync.dma_start(out=w_codes[:], in_=w_words[0])
+                elif nm == "wsc":
+                    for q in range(4):
+                        nc.sync.dma_start(
+                            out=w_sc[32 * q : 32 * q + 4, :].bitcast(I32),
+                            in_=w_scales[0][4 * q : 4 * q + 4, :].bitcast(I32),
+                        )
+                else:
+                    dst, x = big[nm[:-1]]
+                    nc.sync.dma_start(out=dst[int(nm[-1])][:], in_=rows(x, int(nm[-1])))
 
             hf_grp = {}
 
@@ -174,21 +185,20 @@ def tile_persistentmeanfieldisingrbmgradient_w4_kernel(
 
             def weight(u):
                 g, m = u // MT, u % MT
-                h, mm = m // HALF, m % HALF
-                if mm == 0:
-                    v1_grp[(h, g)] = ring.tile(
-                        [P, 2048], BF16, name="v1_grp%d_%d" % (h, g), tag="v1_grp", bufs=4, align_bytes=256
-                    )
+                if m == 0:
+                    v1_grp[g] = ring.tile([P, 4096], BF16, name="v1_grp%d" % g, tag="v1_grp", bufs=2, align_bytes=256)
                 nc.vector.tensor_tensor(
-                    out=v1_grp[(h, g)][:, 512 * mm : 512 * mm + 512].rearrange("p (q t) -> p q t", t=4),
+                    out=v1_grp[g][:, 512 * m : 512 * m + 512].rearrange("p (q t) -> p q t", t=4),
                     in0=t_bank[u][:].rearrange("p t q -> p q t"),
                     in1=s_neg[:, g, :].unsqueeze(1).to_broadcast([P, P, 4]),
                     op=ALU.mult,
                 )
 
-            def v1_quant(h, g):
+            def v1_quant(g, c0, n):
                 nc.vector.quantize_mx(
-                    out=v1_codes[h][g][:].bitcast(E4M3X4), scales=v1_sc[h][g][:], in_=v1_grp[(h, g)][:]
+                    out=v1_codes[g][:, P * c0 : P * (c0 + n)].bitcast(E4M3X4),
+                    scales=v1_sc[g][:, P * c0 : P * (c0 + n)],
+                    in_=v1_grp[g][:, 512 * c0 : 512 * (c0 + n)],
                 )
 
             h_grp = {}
@@ -258,10 +268,10 @@ def tile_persistentmeanfieldisingrbmgradient_w4_kernel(
                     nc.vector.tensor_copy(out=d, in_=sr)
 
             def v_quant(mp, g):
-                c0 = 256 * (mp % 2)
+                c0 = 256 * mp
                 nc.vector.quantize_mx(
-                    out=v_codes[mp // 2][g][:, c0 : c0 + 256].bitcast(E4M3X4),
-                    scales=v_sc[mp // 2][g][:, c0 : c0 + 256],
+                    out=v_codes[g][:, c0 : c0 + 256].bitcast(E4M3X4),
+                    scales=v_sc[g][:, c0 : c0 + 256],
                     in_=v_grp[(mp, g)][:],
                 )
 
@@ -281,10 +291,20 @@ def tile_persistentmeanfieldisingrbmgradient_w4_kernel(
                 for c in range(H // GP_COLS):
                     h_mix_gp(nm, raw, g, GP_COLS * c, GP_COLS)
 
-            mix_gp("n", hn_raw, 0)
+            if not V_N0:
+                mix_gp("n", hn_raw, 0)
             mix_gp("n", hn_raw, 1)
             mix_gp("n", hn_raw, 2)
             mix_gp("n", hn_raw, 3)
+
+            widen_list = [(h, g, t) for h in range(2) for g in range(G) for t in range(4)]
+            done = [0]
+
+            def widen_some(n):
+                for k in range(n):
+                    if done[0] < len(widen_list):
+                        widen(*widen_list[done[0]])
+                        done[0] = done[0] + 1
 
             hf_turn(0, 0)
             hf_turn(0, 1)
@@ -299,31 +319,28 @@ def tile_persistentmeanfieldisingrbmgradient_w4_kernel(
             nc.vector.tensor_scalar(
                 out=s_neg[:], in0=s_bf[:], scalar1=-1.0, scalar2=None, op0=ALU.mult
             )
-            hf_turn(1, 0)
-            hf_turn(1, 1)
-            hf_out(1, 0)
-            hf_out(1, 1)
+            widen_some(HEAD_WIDEN[0])
             for u in range(4):
                 field(u)
+            widen_some(HEAD_WIDEN[1])
+            if V_N0:
+                h_new("n", 0)
+                h_mix_v("n", hn_raw, 0)
             tanh(0)
             tanh(1)
-            hf_quant(1, 0)
-            hf_quant(1, 1)
             mix_gp("p", hp_raw, 0)
             mix_gp("p", hp_raw, 1)
 
-            widen_list = [(h, g, t) for h in range(2) for g in range(G) for t in range(4)]
             hq = [(quant_hn, 0), (quant_hn, 1), (quant_hn, 2), (quant_hn, 3), (quant_hp, 0), (quant_hp, 1), (quant_hp, 2), (quant_hp, 3)]
             nq = 0
-            nw = 0
             npairs = G * MT // 2
             for j in range(npairs):
-                if j < 2:
-                    hf_turn(2 + j, 0)
-                    hf_turn(2 + j, 1)
-                    hf_out(2 + j, 0)
-                    hf_out(2 + j, 1)
-                    hf_quant(2 + j, 0)
+                hg = TR_AT.get(j, 0)
+                if hg:
+                    hf_turn(hg, 0)
+                    hf_turn(hg, 1)
+                    hf_out(hg, 0)
+                    hf_out(hg, 1)
                 turn(2 * j)
                 turn(2 * j + 1)
                 if j + 2 < npairs:
@@ -333,29 +350,31 @@ def tile_persistentmeanfieldisingrbmgradient_w4_kernel(
                     tanh(2 * j + 2)
                     tanh(2 * j + 3)
                 weight(2 * j)
-                if j < 2:
-                    hf_quant(2 + j, 1)
-                if j % 2 == 0 and j > 0:
-                    k = j // 2 - 1
-                    v1_quant(k % 2, k // 2)
+                if hg:
+                    nc.vector.quantize_mx(
+                        out=hf_codes[hg][:].bitcast(E4M3X4), scales=hf_sc[hg][:], in_=hf_grp[hg][:]
+                    )
+                if V1Q == 8 and j % 4 == 0 and j > 0:
+                    v1_quant(j // 4 - 1, 0, 8)
+                if V1Q == 4 and j % 2 == 0 and j > 0:
+                    v1_quant((j - 2) // 4, 4 * ((j - 2) // 2 % 2), 4)
                 weight(2 * j + 1)
                 if j in HQ_AT:
                     hq[nq][0](hq[nq][1])
                     nq = nq + 1
-                for k in range(WIDEN_AT.get(j, 1)):
-                    widen(*widen_list[nw])
-                    nw = nw + 1
-            mix_gp("p", hp_raw, 3)
-            v1_quant(1, G - 1)
+                widen_some(WIDEN_AT.get(j, 1))
+            for g in GP_LATE:
+                mix_gp("p", hp_raw, g)
+            v1_quant(G - 1, 8 - V1Q, V1Q)
 
             acc = [bank("f", [P, H]) for m in range(HALF)] + [bank("t", [P, H]) for m in range(HALF)]
 
             def one_pass(m, codes, sc, rc, rs, g, first, last):
-                c0 = P * (m % HALF)
+                c0 = P * m
                 nc.tensor.matmul_mx(
                     out=acc[m][:],
-                    lhsT=codes[m // HALF][g][:, c0 : c0 + P].bitcast(E4M3X4),
-                    lhsT_scale=sc[m // HALF][g][:, c0 : c0 + P],
+                    lhsT=codes[g][:, c0 : c0 + P].bitcast(E4M3X4),
+                    lhsT_scale=sc[g][:, c0 : c0 + P],
                     rhs=rc[g][:].bitcast(E4M3X4),
                     rhs_scale=rs[g][:],
                     start=first,
@@ -379,19 +398,20 @@ def tile_persistentmeanfieldisingrbmgradient_w4_kernel(
                 for h in range(2):
                     for mm in range(HALF):
                         one_pass(HALF * h + mm, v1_codes, v1_sc, hn_codes, hn_sc, g, g == 0, False)
-            h_mix_s("p", hp_raw, 2)
+            for g in S_HP:
+                h_mix_s("p", hp_raw, g)
             jobs = [(mp, g) for mp in range(4) for g in range(G)]
 
             def mix_job(i):
                 for c in range(2):
                     v_mix(jobs[i][0], jobs[i][1], c)
 
+            for g in V_HP:
+                h_new("p", g)
+                h_mix_v("p", hp_raw, g)
             mix_job(0)
             for i in range(len(jobs)):
-                for k in range(WIDEN_PER_JOB):
-                    if nw < len(widen_list):
-                        widen(*widen_list[nw])
-                        nw = nw + 1
+                widen_some(WIDEN_PER_JOB)
                 if i + 1 < len(jobs):
                     mix_job(i + 1)
                 v_quant(*jobs[i])

from contextlib import ExitStack

import concourse.mybir as mybir
from concourse.masks import make_identity

B, V, H = 2048, 1024, 512
FLOPS = 3 * 2 * B * V * H

F32 = mybir.dt.float32
BF16 = mybir.dt.bfloat16
U32 = mybir.dt.uint32
I32 = mybir.dt.int32
U8 = mybir.dt.uint8
E4M3 = mybir.dt.float8_e4m3fn
E4M3X4 = mybir.dt.float8_e4m3fn_x4
E2M1X4 = mybir.dt.float4_e2m1fn_x4
ACT = mybir.ActivationFunctionType
ALU = mybir.AluOpType

P = 128
G = 4
MT = V // P
HALF = MT // 2
S_SHARE = ((2, 1), (2, 2), (2, 3), (3, 0), (3, 1), (3, 2))
G_SHARE = ((0, 3),)
V_OUT = (5, 6)
STORE_AT = ((0, 13), (1, 13), (2, 14), (3, 14), (4, 15), (5, 15), (6, 15), (7, 15))
WIDEN_PER_JOB = 4
GP_COLS = 128
V1Q = 4
GP_LATE = (3,)
S_HP = (2,)
V_HP = ()
V_N0 = 0
HQ_AT = (2, 7, 14)
WIDEN_AT = {}
TR_AT = {1: 1, 4: 2, 8: 3}
HEAD_WIDEN = (0, 0, 0)
LOADS = ('hf0a', 'hf0b', 'w', 'wsc', 'hn0', 'hf1', 'v0', 'hn1', 'hn3', 'v1', 'hf2', 'hn2', 'hp2', 'v2', 'hp3', 'hp0', 'hf3', 'hp1', 'v3')


def tile_persistentmeanfieldisingrbmgradient_w4_kernel(
    tc, v_bytes, v_scale, hp, hf, hn, w_words, w_scales, b, s, out
):
    nc = tc.nc
    with ExitStack() as ctx:
        keep = ctx.enter_context(tc.tile_pool(name="keep", bufs=1))
        ring = ctx.enter_context(tc.tile_pool(name="ring", bufs=4))
        psum = ctx.enter_context(tc.psum_pool(name="psum", bufs=1))

        def kt(name, shape, dtype):
            return keep.tile(shape, dtype, name=name, align_bytes=256)

        counts = {"f": 0, "t": 0}

        def bank(kind, shape):
            i = counts[kind] % 4
            counts[kind] = counts[kind] + 1
            nm = kind + str(i)
            return psum.tile(shape, F32, name=nm, tag=nm)

        def r4(nm):
            return ring.tile([P, 4, 512], BF16, name=nm, tag="r4", bufs=12, align_bytes=256)

        def grp(nm):
            return ring.tile([P, 2048], BF16, name=nm, tag="grp", bufs=2, align_bytes=256)

        hf_raw = [r4("hf_raw%d" % g) for g in range(G)]
        hn_raw = [r4("hn_raw%d" % g) for g in range(G)]
        hp_raw = [r4("hp_raw%d" % g) for g in range(G)]
        v_raw = [kt("v_raw%d" % g, [P, 4, V], U8) for g in range(G)]
        hf_codes = [kt("hf_codes%d" % g, [P, 512], U32) for g in range(G)]
        hf_sc = [kt("hf_sc%d" % g, [P, 512], U8) for g in range(G)]
        hn_codes = [kt("hn_codes%d" % g, [P, H], U32) for g in range(G)]
        hn_sc = [kt("hn_sc%d" % g, [P, H], U8) for g in range(G)]
        hp_codes = [kt("hp_codes%d" % g, [P, H], U32) for g in range(G)]
        hp_sc = [kt("hp_sc%d" % g, [P, H], U8) for g in range(G)]
        v1_codes = [kt("v1_codes%d" % g, [P, V], U32) for g in range(G)]
        v1_sc = [kt("v1_sc%d" % g, [P, V], U8) for g in range(G)]
        v_codes = [kt("v_codes%d" % g, [P, V], U32) for g in range(G)]
        v_sc = [kt("v_sc%d" % g, [P, V], U8) for g in range(G)]
        w_codes = kt("w_codes", [P, 2 * V], U8)
        w_sc = kt("w_sc", [P, V], U8)
        ident = kt("ident", [P, P], F32)
        b_rows = kt("b_rows", [P, P], BF16)
        b_rows32 = kt("b_rows32", [P, P], F32)
        bias = kt("bias", [P, MT], F32)
        s_bf = kt("s_bf", [P, G, 4], BF16)
        s_neg = kt("s_neg", [P, G, 4], F32)
        vs = kt("vs", [P, G, 4], F32)
        warm = kt("warm", [P, 1], F32)

        with tc.manual_schedule():
            nc.vector.memset(b_rows[:], 0.0)
            nc.vector.memset(w_sc[:].bitcast(I32), 0)
            nc.vector.memset(warm[:], 0.0)
            make_identity(nc, ident[:])
            nc.scalar.dma_start(out=b_rows[0:MT, :], in_=b.rearrange("(m c) -> m c", c=P))
            nc.scalar.dma_start(out=s_bf[:], in_=s.rearrange("(g p t) -> p g t", p=P, t=4))
            nc.gpsimd.dma_start(out=vs[:], in_=v_scale.rearrange("(g p t) o -> p g (t o)", p=P, t=4))
            nc.scalar.activation(warm[:], warm[:], ACT.Tanh)

            def rows(x, g):
                return x.rearrange("(g p t) k -> g p t k", p=P, t=4)[g]

            big = {"hf": (hf_raw, hf), "hn": (hn_raw, hn), "hp": (hp_raw, hp), "v": (v_raw, v_bytes)}
            for nm in LOADS:
                if nm == "hf0a":
                    nc.sync.dma_start(out=hf_raw[0][:, 0:2, :], in_=rows(hf, 0)[:, 0:2, :])
                elif nm == "hf0b":
                    nc.sync.dma_start(out=hf_raw[0][:, 2:4, :], in_=rows(hf, 0)[:, 2:4, :])
                elif nm == "w":
                    nc.sync.dma_start(out=w_codes[:], in_=w_words[0])
                elif nm == "wsc":
                    for q in range(4):
                        nc.sync.dma_start(
                            out=w_sc[32 * q : 32 * q + 4, :].bitcast(I32),
                            in_=w_scales[0][4 * q : 4 * q + 4, :].bitcast(I32),
                        )
                else:
                    dst, x = big[nm[:-1]]
                    nc.sync.dma_start(out=dst[int(nm[-1])][:], in_=rows(x, int(nm[-1])))

            hf_grp = {}

            tr_bank = {}

            def hf_turn(g, h):
                if h == 0:
                    hf_grp[g] = grp("hf_grp%d" % g)
                bk = bank("t", [P, 2, 2, P])
                tr_bank[(g, h)] = bk
                words = hf_raw[g][:].rearrange("p t k -> p (t k)").bitcast(F32)
                for i in range(2):
                    for u in range(2):
                        base = 256 * (2 * h + i)
                        nc.tensor.transpose(bk[:, i, u, :], words[:, base + u : base + 256 : 2], ident[:])

            def hf_out(g, h):
                dst = hf_grp[g][:, 1024 * h : 1024 * h + 1024].bitcast(F32).rearrange(
                    "p (i m u) -> p i m u", i=2, u=2
                )
                src = tr_bank[(g, h)][:].rearrange("p i u m -> p i m u")
                if h == 0:
                    nc.vector.tensor_copy(out=dst, in_=src)
                else:
                    nc.scalar.copy(out=dst, in_=src)

            def hf_quant(g, h):
                nc.vector.quantize_mx(
                    out=hf_codes[g][:, 256 * h : 256 * h + 256].bitcast(E4M3X4),
                    scales=hf_sc[g][:, 256 * h : 256 * h + 256],
                    in_=hf_grp[g][:, 1024 * h : 1024 * h + 1024],
                )

            f_bank = {}
            th = {}
            t_bank = {}
            v1_grp = {}

            def field(u):
                g, m = u // MT, u % MT
                f_bank[u] = bank("f", [P, 512])
                nc.tensor.matmul_mx(
                    out=f_bank[u][:],
                    lhsT=w_codes[:, 256 * m : 256 * m + 256].bitcast(E2M1X4),
                    lhsT_scale=w_sc[:, P * m : P * m + P],
                    rhs=hf_codes[g][:].bitcast(E4M3X4),
                    rhs_scale=hf_sc[g][:],
                    start=True,
                    stop=True,
                )

            def tanh(u):
                m = u % MT
                th[u] = ring.tile([P, 4, P], F32, name="th%d" % u, tag="th", bufs=8)
                nc.scalar.activation(
                    th[u][:].rearrange("p t q -> p (t q)"), f_bank[u][:], ACT.Tanh, bias=bias[:, m : m + 1]
                )

            def turn(u):
                t_bank[u] = bank("t", [P, 4, P])
                for t in range(4):
                    nc.tensor.transpose(t_bank[u][:, t, :], th[u][:, t, :], ident[:])

            def weight(u):
                g, m = u // MT, u % MT
                if m == 0:
                    v1_grp[g] = ring.tile([P, 4096], BF16, name="v1_grp%d" % g, tag="v1_grp", bufs=2, align_bytes=256)
                nc.vector.tensor_tensor(
                    out=v1_grp[g][:, 512 * m : 512 * m + 512].rearrange("p (q t) -> p q t", t=4),
                    in0=t_bank[u][:].rearrange("p t q -> p q t"),
                    in1=s_neg[:, g, :].unsqueeze(1).to_broadcast([P, P, 4]),
                    op=ALU.mult,
                )

            def v1_quant(g, c0, n):
                nc.vector.quantize_mx(
                    out=v1_codes[g][:, P * c0 : P * (c0 + n)].bitcast(E4M3X4),
                    scales=v1_sc[g][:, P * c0 : P * (c0 + n)],
                    in_=v1_grp[g][:, 512 * c0 : 512 * (c0 + n)],
                )

            h_grp = {}

            def h_new(nm, g):
                h_grp[(nm, g)] = ring.tile(
                    [P, 2048], BF16, name="h_grp_%s%d" % (nm, g), tag="h_grp", bufs=6, align_bytes=256
                )

            def h_mix_gp(nm, raw, g, c0, n):
                nc.gpsimd.tensor_scalar(
                    out=h_grp[(nm, g)][:, 4 * c0 : 4 * (c0 + n)].rearrange("p (c t) -> p c t", t=4),
                    in0=raw[g][:, :, c0 : c0 + n].rearrange("p t c -> p c t"),
                    scalar1=1.0,
                    scalar2=0.0,
                    op0=ALU.mult,
                    op1=ALU.add,
                )

            def mix_views(dst, src):
                return (
                    dst.rearrange("p (c i t) -> p c t i", i=4, t=4),
                    src.rearrange("p t (c i) -> p c t i", i=4),
                )

            def h_mix_v(nm, raw, g):
                d, sr = mix_views(h_grp[(nm, g)][:], raw[g][:])
                nc.vector.tensor_copy(out=d, in_=sr)

            def h_quant(nm, codes, sc, g):
                nc.vector.quantize_mx(out=codes[g][:].bitcast(E4M3X4), scales=sc[g][:], in_=h_grp[(nm, g)][:])

            v_wide = {}
            v_grp = {}

            def widen(h, g, t):
                if t == 0:
                    v_wide[(h, g)] = r4("v_wide%d_%d" % (h, g))
                nc.scalar.activation(
                    v_wide[(h, g)][:, t, :],
                    v_raw[g][:, t, 512 * h : 512 * h + 512].bitcast(E4M3),
                    ACT.Copy,
                    scale=vs[:, g, t : t + 1],
                )

            def v_mix(mp, g, c):
                if c == 0:
                    v_grp[(mp, g)] = ring.tile(
                        [P, 1024], BF16, name="v_grp%d_%d" % (mp, g), tag="v_grp", bufs=5, align_bytes=256
                    )
                c0 = P * (2 * (mp % 2) + c)
                dst = v_grp[(mp, g)][:, 512 * c : 512 * c + 512]
                src = v_wide[(mp // 2, g)][:, :, c0 : c0 + P]
                d, sr = mix_views(dst, src)
                if c == 1 and (mp, g) in S_SHARE:
                    nc.scalar.copy(out=d, in_=sr)
                elif (mp, g) in G_SHARE:
                    nc.gpsimd.tensor_scalar(
                        out=dst.rearrange("p (c t) -> p c t", t=4),
                        in0=src.rearrange("p t c -> p c t"),
                        scalar1=1.0,
                        scalar2=0.0,
                        op0=ALU.mult,
                        op1=ALU.add,
                    )
                else:
                    nc.vector.tensor_copy(out=d, in_=sr)

            def v_quant(mp, g):
                c0 = 256 * mp
                nc.vector.quantize_mx(
                    out=v_codes[g][:, c0 : c0 + 256].bitcast(E4M3X4),
                    scales=v_sc[g][:, c0 : c0 + 256],
                    in_=v_grp[(mp, g)][:],
                )

            def h_mix_s(nm, raw, g):
                h_new(nm, g)
                d, sr = mix_views(h_grp[(nm, g)][:], raw[g][:])
                nc.scalar.copy(out=d, in_=sr)

            def quant_hn(g):
                h_quant("n", hn_codes, hn_sc, g)

            def quant_hp(g):
                h_quant("p", hp_codes, hp_sc, g)

            def mix_gp(nm, raw, g):
                h_new(nm, g)
                for c in range(H // GP_COLS):
                    h_mix_gp(nm, raw, g, GP_COLS * c, GP_COLS)

            if not V_N0:
                mix_gp("n", hn_raw, 0)
            mix_gp("n", hn_raw, 1)
            mix_gp("n", hn_raw, 2)
            mix_gp("n", hn_raw, 3)

            widen_list = [(h, g, t) for h in range(2) for g in range(G) for t in range(4)]
            done = [0]

            def widen_some(n):
                for k in range(n):
                    if done[0] < len(widen_list):
                        widen(*widen_list[done[0]])
                        done[0] = done[0] + 1

            hf_turn(0, 0)
            hf_turn(0, 1)
            hf_out(0, 0)
            hf_out(0, 1)
            nc.vector.tensor_copy(out=b_rows32[:], in_=b_rows[:])
            hf_quant(0, 0)
            b_bank = bank("t", [P, P])
            nc.tensor.transpose(b_bank[:], b_rows32[:], ident[:])
            nc.vector.tensor_copy(out=bias[:], in_=b_bank[:, 0:MT])
            hf_quant(0, 1)
            nc.vector.tensor_scalar(
                out=s_neg[:], in0=s_bf[:], scalar1=-1.0, scalar2=None, op0=ALU.mult
            )
            widen_some(HEAD_WIDEN[0])
            for u in range(4):
                field(u)
            widen_some(HEAD_WIDEN[1])
            if V_N0:
                h_new("n", 0)
                h_mix_v("n", hn_raw, 0)
            tanh(0)
            tanh(1)
            mix_gp("p", hp_raw, 0)
            mix_gp("p", hp_raw, 1)

            hq = [(quant_hn, 0), (quant_hn, 1), (quant_hn, 2), (quant_hn, 3), (quant_hp, 0), (quant_hp, 1), (quant_hp, 2), (quant_hp, 3)]
            nq = 0
            npairs = G * MT // 2
            for j in range(npairs):
                hg = TR_AT.get(j, 0)
                if hg:
                    hf_turn(hg, 0)
                    hf_turn(hg, 1)
                    hf_out(hg, 0)
                    hf_out(hg, 1)
                turn(2 * j)
                turn(2 * j + 1)
                if j + 2 < npairs:
                    field(2 * j + 4)
                    field(2 * j + 5)
                if j + 1 < npairs:
                    tanh(2 * j + 2)
                    tanh(2 * j + 3)
                weight(2 * j)
                if hg:
                    nc.vector.quantize_mx(
                        out=hf_codes[hg][:].bitcast(E4M3X4), scales=hf_sc[hg][:], in_=hf_grp[hg][:]
                    )
                if V1Q == 8 and j % 4 == 0 and j > 0:
                    v1_quant(j // 4 - 1, 0, 8)
                if V1Q == 4 and j % 2 == 0 and j > 0:
                    v1_quant((j - 2) // 4, 4 * ((j - 2) // 2 % 2), 4)
                weight(2 * j + 1)
                if j in HQ_AT:
                    hq[nq][0](hq[nq][1])
                    nq = nq + 1
                widen_some(WIDEN_AT.get(j, 1))
            for g in GP_LATE:
                mix_gp("p", hp_raw, g)
            v1_quant(G - 1, 8 - V1Q, V1Q)

            acc = [bank("f", [P, H]) for m in range(HALF)] + [bank("t", [P, H]) for m in range(HALF)]

            def one_pass(m, codes, sc, rc, rs, g, first, last):
                c0 = P * m
                nc.tensor.matmul_mx(
                    out=acc[m][:],
                    lhsT=codes[g][:, c0 : c0 + P].bitcast(E4M3X4),
                    lhsT_scale=sc[g][:, c0 : c0 + P],
                    rhs=rc[g][:].bitcast(E4M3X4),
                    rhs_scale=rs[g][:],
                    start=first,
                    stop=last,
                )

            def store(m):
                res = ring.tile([P, H], F32, name="res%d" % m, tag="th", bufs=8)
                if m in V_OUT:
                    nc.vector.tensor_scalar(
                        out=res[:], in0=acc[m][:], scalar1=float(B) ** -0.5, scalar2=None, op0=ALU.mult
                    )
                else:
                    nc.scalar.activation(res[:], acc[m][:], ACT.Copy, scale=float(B) ** -0.5)
                nc.sync.dma_start(out=out[P * m : P * m + P, :], in_=res[:])

            while nq < 4:
                hq[nq][0](hq[nq][1])
                nq = nq + 1
            for g in range(G):
                for h in range(2):
                    for mm in range(HALF):
                        one_pass(HALF * h + mm, v1_codes, v1_sc, hn_codes, hn_sc, g, g == 0, False)
            for g in S_HP:
                h_mix_s("p", hp_raw, g)
            jobs = [(mp, g) for mp in range(4) for g in range(G)]

            def mix_job(i):
                for c in range(2):
                    v_mix(jobs[i][0], jobs[i][1], c)

            for g in V_HP:
                h_new("p", g)
                h_mix_v("p", hp_raw, g)
            mix_job(0)
            for i in range(len(jobs)):
                widen_some(WIDEN_PER_JOB)
                if i + 1 < len(jobs):
                    mix_job(i + 1)
                v_quant(*jobs[i])
                if nq < len(hq):
                    hq[nq][0](hq[nq][1])
                    nq = nq + 1
                mp, g = jobs[i]
                for c in range(2):
                    one_pass(2 * mp + c, v_codes, v_sc, hp_codes, hp_sc, g, False, g == G - 1)
                for (m, at) in STORE_AT:
                    if at == i:
                        store(m)
